import numpy as np, ml_dtypes
CORES = [9,13,81,85,89,93,97,101,113,117,121,125]
N = 12
KB, QP = 2, 64
MEM = [2,5]
def setup_inputs(rng):
    return {"q": rng.standard_normal((N, 128, QP), dtype=np.float32).astype(ml_dtypes.bfloat16), "k": rng.standard_normal((N, 128, KB * 128), dtype=np.float32).astype(ml_dtypes.bfloat16), "v": rng.standard_normal((N, 128, KB * 128), dtype=np.float32).astype(ml_dtypes.bfloat16)}
def setup_inputs_big(rng):
    d = setup_inputs(rng)
    for k in ("q", "k", "v"): d[k] = (d[k].astype(np.float32) * 1024.0).astype(d[k].dtype)
    return d
def setup_inputs_small(rng):
    d = setup_inputs(rng)
    for k in ("q", "k", "v"): d[k] = (d[k].astype(np.float32) * (1 / 1024.0)).astype(d[k].dtype)
    return d
def setup_inputs_apart(rng):
    d = setup_inputs(rng)
    f = (10.0 ** rng.permutation(np.linspace(-1.5, 1.5, N))).astype(np.float32).reshape(N, 1, 1)
    for k in ("q", "k", "v"): d[k] = (d[k].astype(np.float32) * f).astype(d[k].dtype)
    return d
def reference(q, k, v):
    Q, K, V = q.astype(np.float64), k.astype(np.float64), v.astype(np.float64)
    y = np.zeros((N, 128, QP))
    for r in range(N):
        for j in MEM:
            for b in range(KB):
                S = np.maximum(K[j][:, 128 * b:128 * b + 128].T @ Q[r], 0.0)
                y[r] += V[j][:, 128 * b:128 * b + 128].T @ S
    return {"y": y.astype(ml_dtypes.bfloat16 if q.dtype != np.float64 else np.float64)}

@@ -1,0 +1,186 @@
+from concourse.bass import DstId, RemoteDMATransfer
+from concourse.mybir import dt, AluOpType
+
+QP = 64
+KW = 128
+NSRV = 3
+NQ = 8
+NF = 8
+GW = 128
+
+SCRATCH = {
+    "qsb": ("sbuf", [128, QP], "bfloat16"),
+    "kv": ("sbuf", [128, 4 * KW], "bfloat16"),
+    "qn": ("sbuf", [128, GW], "bfloat16"),
+    "qf": ("sbuf", [128, GW], "bfloat16"),
+    "zero": ("sbuf", [128, GW], "float32"),
+    "sn0": ("sbuf", [128, GW], "bfloat16"),
+    "sn1": ("sbuf", [128, GW], "bfloat16"),
+    "sf0": ("sbuf", [128, GW], "bfloat16"),
+    "sf1": ("sbuf", [128, GW], "bfloat16"),
+    "on": ("sbuf", [128, GW], "bfloat16"),
+    "of": ("sbuf", [128, GW], "bfloat16"),
+    "part": ("sbuf", [128, 2 * QP], "bfloat16"),
+    "ysb": ("sbuf", [128, QP], "bfloat16"),
+    "pn0": ("psum", [128, 512], "float32"),
+    "pn1": ("psum", [128, 512], "float32"),
+    "pno": ("psum", [128, 512], "float32"),
+    "pf0": ("psum", [128, 512], "float32"),
+    "pf1": ("psum", [128, 512], "float32"),
+    "pfo": ("psum", [128, 512], "float32"),
+}
+SEMAPHORES = ["ldq", "ldk", "ldv", "sent", "ka", "va", "qna", "qfa", "z",
+              "tn0", "tn1", "rn0", "rn1", "tno", "cn",
+              "tf0", "tf1", "rf0", "rf1", "tfo", "cf",
+              "pa", "ad", "st"]
+
+
+def _take(mask, n, skip=0):
+    bits = [b for b in range(mask.bit_length()) if (mask >> b) & 1]
+    m = 0
+    for b in bits[skip:skip + n]:
+        m |= 1 << b
+    return m
+
+
+def _count(mask):
+    return sum((mask >> b) & 1 for b in range(mask.bit_length()))
+
+
+def _share(n_engines, n_dst):
+    per = 1
+    while per * 2 * n_dst <= n_engines:
+        per *= 2
+    return per
+
+
+def _plan(T, topo):
+    cores = list(T.cores)
+    mem = [cores[j] for j in T.tables["MEM"]]
+    every = range(topo.CHIPS * topo.CORES_PER_CHIP)
+    servers, groups = [], []
+    for a in range(2):
+        m, other = mem[a], mem[1 - a]
+        own = [c for c in every
+               if topo.chip(c) == topo.chip(m) and c not in cores and topo.may_write(c, other)]
+        dies = sorted(set(topo.die(c) for c in own))
+        per_die = [[c for c in own if topo.die(c) == d] for d in dies]
+        order = [l[i] for i in range(max(len(l) for l in per_die)) for l in per_die if i < len(l)]
+        servers.append(order[:NSRV])
+        near = [c for c in cores if c == m or topo.may_write(c, m)]
+        size = -(-len(near) // NSRV)
+        groups.append([near[i * size:(i + 1) * size] for i in range(NSRV)])
+    return mem, servers, groups
+
+
+def _dst(topo, c):
+    rid, pid, _ = topo.addr(c)
+    return DstId(rid=rid, pnc=pid)
+
+
+def rank_program(g, core, T, topo):
+    mem, servers, groups = _plan(T, topo)
+    sem = T.sem
+    sent = 0
+
+    if T.rank_of(core) is not None:
+        side = [a for a in range(2) if any(core in grp for grp in groups[a])][0]
+        gi = [i for i in range(NSRV) if core in groups[side][i]][0]
+        slot = groups[side][gi].index(core)
+        srv, far_srv = servers[side][gi], servers[1 - side][gi]
+        is_mem = core == mem[side]
+
+        g.sync.dma_start(T.qsb[:], T.q[:]).then_inc(sem.ldq, 16)
+        if is_mem:
+            g.scalar.dma_start(T.kv[:, 0:2 * KW], T.k[:]).then_inc(sem.ldk, 16)
+            g.sync.dma_start(T.kv[:, 2 * KW:4 * KW], T.v[:]).then_inc(sem.ldv, 16)
+
+        g.wait_ge(sem.ldq, 16)
+        rid, pid, _ = topo.addr(srv)
+        g.remote_dma(out_ap=T.qn[:, QP * slot:QP * slot + QP], in_ap=T.qsb[:], remote_sem=sem.qna,
+                     local_sem=sem.sent, pid=pid, routing_id=rid,
+                     dma_engine_mask=_take(topo.mask(core, srv), NQ))
+        sent += NQ
+
+        if is_mem:
+            common = topo.mask(core, servers[side][0])
+            for s in servers[side]:
+                common &= topo.mask(core, s)
+            for lo, ld, arr in ((0, sem.ldk, sem.ka), (2 * KW, sem.ldv, sem.va)):
+                g.wait_ge(ld, 16)
+                piece = T.kv[:, lo:lo + 2 * KW]
+                g.remote_dma_fused([RemoteDMATransfer(
+                    dst_ids=[_dst(topo, s) for s in servers[side]], dma_engine_mask=common, remote_sem=arr,
+                    srcs=[piece], dsts=[piece for s in servers[side]], alu_op=0)], local_sem=sem.sent)
+                sent += _count(common)
+
+        n_near = _share(_count(_res_mask(topo, srv, groups[side][gi])), len(groups[side][gi]))
+        n_far = _share(_count(_res_mask(topo, far_srv, groups[side][gi])), len(groups[side][gi]))
+        g.vector.wait_ge(sem.pa, n_near + n_far)
+        g.vector.tensor_tensor(T.ysb[:], T.part[:, 0:QP], T.part[:, QP:2 * QP], AluOpType.add).then_inc(sem.ad, 1)
+        g.sync.wait_ge(sem.ad, 1)
+        g.sync.dma_start(T.y[:], T.ysb[:]).then_inc(sem.st, 16)
+        g.sync.wait_ge(sem.st, 16)
+        g.wait_ge(sem.sent, sent)
+        return
+
+    here = [(a, i) for a in range(2) for i in range(NSRV) if servers[a][i] == core]
+    if not here:
+        return
+    side, gi = here[0]
+    twin = servers[1 - side][gi]
+    near, far = groups[side][gi], groups[1 - side][gi]
+    n_kv = topo.mask(mem[side], servers[side][0])
+    for s in servers[side]:
+        n_kv &= topo.mask(mem[side], s)
+    n_kv = _count(n_kv)
+    TE, V = g.tensor, g.vector
+
+    V.memset(T.zero[:], 0.0).then_inc(sem.z, 1)
+    V.wait_ge(sem.z, 1)
+
+    wn = QP * len(near)
+    g.wait_ge(sem.qna, NQ * len(near))
+    rid, pid, _ = topo.addr(twin)
+    g.remote_dma(out_ap=T.qf[:, 0:wn], in_ap=T.qn[:, 0:wn], remote_sem=sem.qfa, local_sem=sem.sent,
+                 pid=pid, routing_id=rid, dma_engine_mask=_take(topo.mask(core, twin), NF))
+    sent += NF
+
+    for tag, grp, qsem, qcnt, col in (("n", near, sem.qna, NQ * len(near), 0), ("f", far, sem.qfa, NF, QP)):
+        w = QP * len(grp)
+        q = T["q" + tag][:, 0:w]
+        p0, p1, po = T["p" + tag + "0"][:, 0:w], T["p" + tag + "1"][:, 0:w], T["p" + tag + "o"][:, 0:w]
+        s0, s1, o = T["s" + tag + "0"][:, 0:w], T["s" + tag + "1"][:, 0:w], T["o" + tag]
+        t0, t1, r0, r1 = sem["t" + tag + "0"], sem["t" + tag + "1"], sem["r" + tag + "0"], sem["r" + tag + "1"]
+        to, c = sem["t" + tag + "o"], sem["c" + tag]
+        TE.wait_ge(sem.ka, n_kv)
+        TE.wait_ge(qsem, qcnt)
+        TE.matmul(p0, T.kv[:, 0:KW], q, True, True).then_inc(t0, 1)
+        TE.matmul(p1, T.kv[:, KW:2 * KW], q, True, True).then_inc(t1, 1)
+        V.wait_ge(t0, 1)
+        V.tensor_tensor(s0, p0, T.zero[:, 0:w], AluOpType.max).then_inc(r0, 1)
+        V.wait_ge(t1, 1)
+        V.tensor_tensor(s1, p1, T.zero[:, 0:w], AluOpType.max).then_inc(r1, 1)
+        TE.wait_ge(sem.va, n_kv)
+        TE.wait_ge(r0, 1)
+        TE.matmul(po, T.kv[:, 2 * KW:3 * KW], s0, True, False)
+        TE.wait_ge(r1, 1)
+        TE.matmul(po, T.kv[:, 3 * KW:4 * KW], s1, False, True).then_inc(to, 1)
+        V.wait_ge(to, 1)
+        V.tensor_copy(o[:, 0:w], po).then_inc(c, 1)
+        avail = _res_mask(topo, core, grp)
+        per = _share(_count(avail), len(grp))
+        g.wait_ge(c, 1)
+        g.remote_dma_fused([RemoteDMATransfer(
+            dst_ids=[_dst(topo, r)], dma_engine_mask=_take(avail, per, per * j), remote_sem=sem.pa,
+            src=o[:, QP * j:QP * j + QP], dst=T.part[:, col:col + QP], alu_op=0)
+            for j, r in enumerate(grp)], local_sem=sem.sent)
+        sent += per * len(grp)
+    g.wait_ge(sem.sent, sent)
+
+
+def _res_mask(topo, srv, grp):
+    m = topo.mask(srv, grp[0])
+    for r in grp:
+        m &= topo.mask(srv, r)
+    return _take(m, NF)

@@ -3,13 +3,15 @@ from concourse.mybir import dt, AluOpType
 
 QP = 64
 KW = 128
-NSRV = 3
 NQ = 8
 NF = 8
+NR = 8
 GW = 128
 
 SCRATCH = {
-    "qsb": ("sbuf", [128, QP], "bfloat16"),
+    "qd": ("dram", [128, QP], "bfloat16"),
+    "kd": ("dram", [128, 2 * KW], "bfloat16"),
+    "vd": ("dram", [128, 2 * KW], "bfloat16"),
     "kv": ("sbuf", [128, 4 * KW], "bfloat16"),
     "qn": ("sbuf", [128, GW], "bfloat16"),
     "qf": ("sbuf", [128, GW], "bfloat16"),
@@ -28,10 +30,11 @@ SCRATCH = {
     "pf0": ("psum", [128, 512], "float32"),
     "pf1": ("psum", [128, 512], "float32"),
     "pfo": ("psum", [128, 512], "float32"),
+    "pfp": ("psum", [128, 512], "float32"),
 }
 SEMAPHORES = ["ldq", "ldk", "ldv", "sent", "ka", "va", "qna", "qfa", "z",
               "tn0", "tn1", "rn0", "rn1", "tno", "cn",
-              "tf0", "tf1", "rf0", "rf1", "tfo", "cf",
+              "t00", "t01", "t10", "t11", "r00", "r01", "r10", "r11", "to0", "to1", "c0", "c1",
               "pa", "ad", "st"]
 
 
@@ -63,13 +66,16 @@ def _plan(T, topo):
         m, other = mem[a], mem[1 - a]
         own = [c for c in every
                if topo.chip(c) == topo.chip(m) and c not in cores and topo.may_write(c, other)]
-        dies = sorted(set(topo.die(c) for c in own))
-        per_die = [[c for c in own if topo.die(c) == d] for d in dies]
-        order = [l[i] for i in range(max(len(l) for l in per_die)) for l in per_die if i < len(l)]
-        servers.append(order[:NSRV])
         near = [c for c in cores if c == m or topo.may_write(c, m)]
-        size = -(-len(near) // NSRV)
-        groups.append([near[i * size:(i + 1) * size] for i in range(NSRV)])
+        srv, grp = [], []
+        for d in sorted(set(topo.die(c) for c in own)):
+            two = [c for c in own if topo.die(c) == d][:2]
+            mine = [c for c in near if topo.die(c) == d]
+            cut = len(mine) - len(mine) // 2 if a == 0 else len(mine) // 2
+            srv += two
+            grp += [mine[:cut], mine[cut:]]
+        servers.append(srv)
+        groups.append(grp)
     return mem, servers, groups
 
 
@@ -78,26 +84,44 @@ def _dst(topo, c):
     return DstId(rid=rid, pnc=pid)
 
 
+def _res_mask(topo, srv, grp):
+    m = topo.mask(srv, grp[0])
+    for r in grp:
+        m &= topo.mask(srv, r)
+    return _take(m, NR)
+
+
+def _give_back(g, T, topo, core, grp, o, col):
+    avail = _res_mask(topo, core, grp)
+    per = _share(_count(avail), len(grp))
+    g.remote_dma_fused([RemoteDMATransfer(
+        dst_ids=[_dst(topo, r)], dma_engine_mask=_take(avail, per, per * j), remote_sem=T.sem.pa,
+        src=o[:, QP * j:QP * j + QP], dst=T.part[:, col:col + QP], alu_op=0)
+        for j, r in enumerate(grp)], local_sem=T.sem.sent)
+    return per * len(grp)
+
+
 def rank_program(g, core, T, topo):
     mem, servers, groups = _plan(T, topo)
+    nsrv = len(servers[0])
     sem = T.sem
     sent = 0
 
     if T.rank_of(core) is not None:
         side = [a for a in range(2) if any(core in grp for grp in groups[a])][0]
-        gi = [i for i in range(NSRV) if core in groups[side][i]][0]
+        gi = [i for i in range(nsrv) if core in groups[side][i]][0]
         slot = groups[side][gi].index(core)
         srv, far_srv = servers[side][gi], servers[1 - side][gi]
         is_mem = core == mem[side]
 
-        g.sync.dma_start(T.qsb[:], T.q[:]).then_inc(sem.ldq, 16)
+        g.sync.dma_start(T.qd[:], T.q[:]).then_inc(sem.ldq, 16)
         if is_mem:
-            g.scalar.dma_start(T.kv[:, 0:2 * KW], T.k[:]).then_inc(sem.ldk, 16)
-            g.sync.dma_start(T.kv[:, 2 * KW:4 * KW], T.v[:]).then_inc(sem.ldv, 16)
+            g.scalar.dma_start(T.kd[:], T.k[:]).then_inc(sem.ldk, 16)
+            g.sync.dma_start(T.vd[:], T.v[:]).then_inc(sem.ldv, 16)
 
         g.wait_ge(sem.ldq, 16)
         rid, pid, _ = topo.addr(srv)
-        g.remote_dma(out_ap=T.qn[:, QP * slot:QP * slot + QP], in_ap=T.qsb[:], remote_sem=sem.qna,
+        g.remote_dma(out_ap=T.qn[:, QP * slot:QP * slot + QP], in_ap=T.qd[:], remote_sem=sem.qna,
                      local_sem=sem.sent, pid=pid, routing_id=rid,
                      dma_engine_mask=_take(topo.mask(core, srv), NQ))
         sent += NQ
@@ -106,12 +130,12 @@ def rank_program(g, core, T, topo):
             common = topo.mask(core, servers[side][0])
             for s in servers[side]:
                 common &= topo.mask(core, s)
-            for lo, ld, arr in ((0, sem.ldk, sem.ka), (2 * KW, sem.ldv, sem.va)):
+            for lo, stage, ld, arr in ((0, T.kd, sem.ldk, sem.ka), (2 * KW, T.vd, sem.ldv, sem.va)):
                 g.wait_ge(ld, 16)
-                piece = T.kv[:, lo:lo + 2 * KW]
                 g.remote_dma_fused([RemoteDMATransfer(
                     dst_ids=[_dst(topo, s) for s in servers[side]], dma_engine_mask=common, remote_sem=arr,
-                    srcs=[piece], dsts=[piece for s in servers[side]], alu_op=0)], local_sem=sem.sent)
+                    srcs=[stage[:]], dsts=[T.kv[:, lo:lo + 2 * KW] for s in servers[side]], alu_op=0)],
+                    local_sem=sem.sent)
                 sent += _count(common)
 
         n_near = _share(_count(_res_mask(topo, srv, groups[side][gi])), len(groups[side][gi]))
@@ -124,7 +148,7 @@ def rank_program(g, core, T, topo):
         g.wait_ge(sem.sent, sent)
         return
 
-    here = [(a, i) for a in range(2) for i in range(NSRV) if servers[a][i] == core]
+    here = [(a, i) for a in range(2) for i in range(nsrv) if servers[a][i] == core]
     if not here:
         return
     side, gi = here[0]
@@ -135,6 +159,8 @@ def rank_program(g, core, T, topo):
         n_kv &= topo.mask(mem[side], s)
     n_kv = _count(n_kv)
     TE, V = g.tensor, g.vector
+    kb = [T.kv[:, 0:KW], T.kv[:, KW:2 * KW]]
+    vb = [T.kv[:, 2 * KW:3 * KW], T.kv[:, 3 * KW:4 * KW]]
 
     V.memset(T.zero[:], 0.0).then_inc(sem.z, 1)
     V.wait_ge(sem.z, 1)
@@ -146,41 +172,46 @@ def rank_program(g, core, T, topo):
                  pid=pid, routing_id=rid, dma_engine_mask=_take(topo.mask(core, twin), NF))
     sent += NF
 
-    for tag, grp, qsem, qcnt, col in (("n", near, sem.qna, NQ * len(near), 0), ("f", far, sem.qfa, NF, QP)):
-        w = QP * len(grp)
-        q = T["q" + tag][:, 0:w]
-        p0, p1, po = T["p" + tag + "0"][:, 0:w], T["p" + tag + "1"][:, 0:w], T["p" + tag + "o"][:, 0:w]
-        s0, s1, o = T["s" + tag + "0"][:, 0:w], T["s" + tag + "1"][:, 0:w], T["o" + tag]
-        t0, t1, r0, r1 = sem["t" + tag + "0"], sem["t" + tag + "1"], sem["r" + tag + "0"], sem["r" + tag + "1"]
-        to, c = sem["t" + tag + "o"], sem["c" + tag]
-        TE.wait_ge(sem.ka, n_kv)
-        TE.wait_ge(qsem, qcnt)
-        TE.matmul(p0, T.kv[:, 0:KW], q, True, True).then_inc(t0, 1)
-        TE.matmul(p1, T.kv[:, KW:2 * KW], q, True, True).then_inc(t1, 1)
-        V.wait_ge(t0, 1)
-        V.tensor_tensor(s0, p0, T.zero[:, 0:w], AluOpType.max).then_inc(r0, 1)
-        V.wait_ge(t1, 1)
-        V.tensor_tensor(s1, p1, T.zero[:, 0:w], AluOpType.max).then_inc(r1, 1)
-        TE.wait_ge(sem.va, n_kv)
-        TE.wait_ge(r0, 1)
-        TE.matmul(po, T.kv[:, 2 * KW:3 * KW], s0, True, False)
-        TE.wait_ge(r1, 1)
-        TE.matmul(po, T.kv[:, 3 * KW:4 * KW], s1, False, True).then_inc(to, 1)
-        V.wait_ge(to, 1)
-        V.tensor_copy(o[:, 0:w], po).then_inc(c, 1)
-        avail = _res_mask(topo, core, grp)
-        per = _share(_count(avail), len(grp))
-        g.wait_ge(c, 1)
-        g.remote_dma_fused([RemoteDMATransfer(
-            dst_ids=[_dst(topo, r)], dma_engine_mask=_take(avail, per, per * j), remote_sem=sem.pa,
-            src=o[:, QP * j:QP * j + QP], dst=T.part[:, col:col + QP], alu_op=0)
-            for j, r in enumerate(grp)], local_sem=sem.sent)
-        sent += per * len(grp)
+    q = T.qn[:, 0:wn]
+    pn, sn = [T.pn0[:, 0:wn], T.pn1[:, 0:wn]], [T.sn0[:, 0:wn], T.sn1[:, 0:wn]]
+    tn, rn = [sem.tn0, sem.tn1], [sem.rn0, sem.rn1]
+    TE.wait_ge(sem.ka, n_kv)
+    TE.wait_ge(sem.qna, NQ * len(near))
+    for b in range(2):
+        TE.matmul(pn[b], kb[b], q, True, True).then_inc(tn[b], 1)
+        V.wait_ge(tn[b], 1)
+        V.tensor_tensor(sn[b], pn[b], T.zero[:, 0:wn], AluOpType.max).then_inc(rn[b], 1)
+    TE.wait_ge(sem.va, n_kv)
+    TE.wait_ge(rn[0], 1)
+    TE.matmul(T.pno[:, 0:wn], vb[0], sn[0], True, False)
+    TE.wait_ge(rn[1], 1)
+    TE.matmul(T.pno[:, 0:wn], vb[1], sn[1], False, True).then_inc(sem.tno, 1)
+    V.wait_ge(sem.tno, 1)
+    V.tensor_copy(T.on[:, 0:wn], T.pno[:, 0:wn]).then_inc(sem.cn, 1)
+    g.wait_ge(sem.cn, 1)
+    sent += _give_back(g, T, topo, core, near, T.on, 0)
+
+    banks = [([T.pf0, T.pf1], T.pfo), ([T.pn0, T.pn1], T.pfp)]
+    sf = [T.sf0, T.sf1]
+    TE.wait_ge(sem.qfa, NF)
+    for j in range(len(far)):
+        lo = QP * j
+        for b in range(2):
+            p = banks[j][0][b][:, 0:QP]
+            TE.matmul(p, kb[b], T.qf[:, lo:lo + QP], True, True).then_inc(sem["t%d%d" % (j, b)], 1)
+            V.wait_ge(sem["t%d%d" % (j, b)], 1)
+            V.tensor_tensor(sf[b][:, lo:lo + QP], p, T.zero[:, 0:QP], AluOpType.max).then_inc(
+                sem["r%d%d" % (j, b)], 1)
+    for j in range(len(far)):
+        lo = QP * j
+        po = banks[j][1][:, 0:QP]
+        TE.wait_ge(sem["r%d0" % j], 1)
+        TE.matmul(po, vb[0], sf[0][:, lo:lo + QP], True, False)
+        TE.wait_ge(sem["r%d1" % j], 1)
+        TE.matmul(po, vb[1], sf[1][:, lo:lo + QP], False, True).then_inc(sem["to%d" % j], 1)
+        V.wait_ge(sem["to%d" % j], 1)
+        V.tensor_copy(T.of[:, lo:lo + QP], po).then_inc(sem["c%d" % j], 1)
+    for j in range(len(far)):
+        g.wait_ge(sem["c%d" % j], 1)
+    sent += _give_back(g, T, topo, core, far, T.of, QP)
     g.wait_ge(sem.sent, sent)
-
-
-def _res_mask(topo, srv, grp):
-    m = topo.mask(srv, grp[0])
-    for r in grp:
-        m &= topo.mask(srv, r)
-    return _take(m, NF)

from concourse.bass import DstId, RemoteDMATransfer
from concourse.mybir import dt, AluOpType

QP = 64
KW = 128
NQ = 8
NF = 8
NR = 8
GW = 128

SCRATCH = {
    "qd": ("dram", [128, QP], "bfloat16"),
    "kd": ("dram", [128, 2 * KW], "bfloat16"),
    "vd": ("dram", [128, 2 * KW], "bfloat16"),
    "kv": ("sbuf", [128, 4 * KW], "bfloat16"),
    "qn": ("sbuf", [128, GW], "bfloat16"),
    "qf": ("sbuf", [128, GW], "bfloat16"),
    "zero": ("sbuf", [128, GW], "float32"),
    "sn0": ("sbuf", [128, GW], "bfloat16"),
    "sn1": ("sbuf", [128, GW], "bfloat16"),
    "sf0": ("sbuf", [128, GW], "bfloat16"),
    "sf1": ("sbuf", [128, GW], "bfloat16"),
    "on": ("sbuf", [128, GW], "bfloat16"),
    "of": ("sbuf", [128, GW], "bfloat16"),
    "part": ("sbuf", [128, 2 * QP], "bfloat16"),
    "ysb": ("sbuf", [128, QP], "bfloat16"),
    "pn0": ("psum", [128, 512], "float32"),
    "pn1": ("psum", [128, 512], "float32"),
    "pno": ("psum", [128, 512], "float32"),
    "pf0": ("psum", [128, 512], "float32"),
    "pf1": ("psum", [128, 512], "float32"),
    "pfo": ("psum", [128, 512], "float32"),
    "pfp": ("psum", [128, 512], "float32"),
}
SEMAPHORES = ["ldq", "ldk", "ldv", "sent", "ka", "va", "qna", "qfa", "z",
              "tn0", "tn1", "rn0", "rn1", "tno", "cn",
              "t00", "t01", "t10", "t11", "r00", "r01", "r10", "r11", "to0", "to1", "c0", "c1",
              "pa", "ad", "st"]


def _take(mask, n, skip=0):
    bits = [b for b in range(mask.bit_length()) if (mask >> b) & 1]
    m = 0
    for b in bits[skip:skip + n]:
        m |= 1 << b
    return m


def _count(mask):
    return sum((mask >> b) & 1 for b in range(mask.bit_length()))


def _share(n_engines, n_dst):
    per = 1
    while per * 2 * n_dst <= n_engines:
        per *= 2
    return per


def _plan(T, topo):
    cores = list(T.cores)
    mem = [cores[j] for j in T.tables["MEM"]]
    every = range(topo.CHIPS * topo.CORES_PER_CHIP)
    servers, groups = [], []
    for a in range(2):
        m, other = mem[a], mem[1 - a]
        own = [c for c in every
               if topo.chip(c) == topo.chip(m) and c not in cores and topo.may_write(c, other)]
        near = [c for c in cores if c == m or topo.may_write(c, m)]
        srv, grp = [], []
        for d in sorted(set(topo.die(c) for c in own)):
            two = [c for c in own if topo.die(c) == d][:2]
            mine = [c for c in near if topo.die(c) == d]
            cut = len(mine) - len(mine) // 2 if a == 0 else len(mine) // 2
            srv += two
            grp += [mine[:cut], mine[cut:]]
        servers.append(srv)
        groups.append(grp)
    return mem, servers, groups


def _dst(topo, c):
    rid, pid, _ = topo.addr(c)
    return DstId(rid=rid, pnc=pid)


def _res_mask(topo, srv, grp):
    m = topo.mask(srv, grp[0])
    for r in grp:
        m &= topo.mask(srv, r)
    return _take(m, NR)


def _give_back(g, T, topo, core, grp, o, col):
    avail = _res_mask(topo, core, grp)
    per = _share(_count(avail), len(grp))
    g.remote_dma_fused([RemoteDMATransfer(
        dst_ids=[_dst(topo, r)], dma_engine_mask=_take(avail, per, per * j), remote_sem=T.sem.pa,
        src=o[:, QP * j:QP * j + QP], dst=T.part[:, col:col + QP], alu_op=0)
        for j, r in enumerate(grp)], local_sem=T.sem.sent)
    return per * len(grp)


def rank_program(g, core, T, topo):
    mem, servers, groups = _plan(T, topo)
    nsrv = len(servers[0])
    sem = T.sem
    sent = 0

    if T.rank_of(core) is not None:
        side = [a for a in range(2) if any(core in grp for grp in groups[a])][0]
        gi = [i for i in range(nsrv) if core in groups[side][i]][0]
        slot = groups[side][gi].index(core)
        srv, far_srv = servers[side][gi], servers[1 - side][gi]
        is_mem = core == mem[side]

        g.sync.dma_start(T.qd[:], T.q[:]).then_inc(sem.ldq, 16)
        if is_mem:
            g.scalar.dma_start(T.kd[:], T.k[:]).then_inc(sem.ldk, 16)
            g.sync.dma_start(T.vd[:], T.v[:]).then_inc(sem.ldv, 16)

        g.wait_ge(sem.ldq, 16)
        rid, pid, _ = topo.addr(srv)
        g.remote_dma(out_ap=T.qn[:, QP * slot:QP * slot + QP], in_ap=T.qd[:], remote_sem=sem.qna,
                     local_sem=sem.sent, pid=pid, routing_id=rid,
                     dma_engine_mask=_take(topo.mask(core, srv), NQ))
        sent += NQ

        if is_mem:
            common = topo.mask(core, servers[side][0])
            for s in servers[side]:
                common &= topo.mask(core, s)
            for lo, stage, ld, arr in ((0, T.kd, sem.ldk, sem.ka), (2 * KW, T.vd, sem.ldv, sem.va)):
                g.wait_ge(ld, 16)
                g.remote_dma_fused([RemoteDMATransfer(
                    dst_ids=[_dst(topo, s) for s in servers[side]], dma_engine_mask=common, remote_sem=arr,
                    srcs=[stage[:]], dsts=[T.kv[:, lo:lo + 2 * KW] for s in servers[side]], alu_op=0)],
                    local_sem=sem.sent)
                sent += _count(common)

        n_near = _share(_count(_res_mask(topo, srv, groups[side][gi])), len(groups[side][gi]))
        n_far = _share(_count(_res_mask(topo, far_srv, groups[side][gi])), len(groups[side][gi]))
        g.vector.wait_ge(sem.pa, n_near + n_far)
        g.vector.tensor_tensor(T.ysb[:], T.part[:, 0:QP], T.part[:, QP:2 * QP], AluOpType.add).then_inc(sem.ad, 1)
        g.sync.wait_ge(sem.ad, 1)
        g.sync.dma_start(T.y[:], T.ysb[:]).then_inc(sem.st, 16)
        g.sync.wait_ge(sem.st, 16)
        g.wait_ge(sem.sent, sent)
        return

    here = [(a, i) for a in range(2) for i in range(nsrv) if servers[a][i] == core]
    if not here:
        return
    side, gi = here[0]
    twin = servers[1 - side][gi]
    near, far = groups[side][gi], groups[1 - side][gi]
    n_kv = topo.mask(mem[side], servers[side][0])
    for s in servers[side]:
        n_kv &= topo.mask(mem[side], s)
    n_kv = _count(n_kv)
    TE, V = g.tensor, g.vector
    kb = [T.kv[:, 0:KW], T.kv[:, KW:2 * KW]]
    vb = [T.kv[:, 2 * KW:3 * KW], T.kv[:, 3 * KW:4 * KW]]

    V.memset(T.zero[:], 0.0).then_inc(sem.z, 1)
    V.wait_ge(sem.z, 1)

    wn = QP * len(near)
    g.wait_ge(sem.qna, NQ * len(near))
    rid, pid, _ = topo.addr(twin)
    g.remote_dma(out_ap=T.qf[:, 0:wn], in_ap=T.qn[:, 0:wn], remote_sem=sem.qfa, local_sem=sem.sent,
                 pid=pid, routing_id=rid, dma_engine_mask=_take(topo.mask(core, twin), NF))
    sent += NF

    q = T.qn[:, 0:wn]
    pn, sn = [T.pn0[:, 0:wn], T.pn1[:, 0:wn]], [T.sn0[:, 0:wn], T.sn1[:, 0:wn]]
    tn, rn = [sem.tn0, sem.tn1], [sem.rn0, sem.rn1]
    TE.wait_ge(sem.ka, n_kv)
    TE.wait_ge(sem.qna, NQ * len(near))
    for b in range(2):
        TE.matmul(pn[b], kb[b], q, True, True).then_inc(tn[b], 1)
        V.wait_ge(tn[b], 1)
        V.tensor_tensor(sn[b], pn[b], T.zero[:, 0:wn], AluOpType.max).then_inc(rn[b], 1)
    TE.wait_ge(sem.va, n_kv)
    TE.wait_ge(rn[0], 1)
    TE.matmul(T.pno[:, 0:wn], vb[0], sn[0], True, False)
    TE.wait_ge(rn[1], 1)
    TE.matmul(T.pno[:, 0:wn], vb[1], sn[1], False, True).then_inc(sem.tno, 1)
    V.wait_ge(sem.tno, 1)
    V.tensor_copy(T.on[:, 0:wn], T.pno[:, 0:wn]).then_inc(sem.cn, 1)
    g.wait_ge(sem.cn, 1)
    sent += _give_back(g, T, topo, core, near, T.on, 0)

    banks = [([T.pf0, T.pf1], T.pfo), ([T.pn0, T.pn1], T.pfp)]
    sf = [T.sf0, T.sf1]
    TE.wait_ge(sem.qfa, NF)
    for j in range(len(far)):
        lo = QP * j
        for b in range(2):
            p = banks[j][0][b][:, 0:QP]
            TE.matmul(p, kb[b], T.qf[:, lo:lo + QP], True, True).then_inc(sem["t%d%d" % (j, b)], 1)
            V.wait_ge(sem["t%d%d" % (j, b)], 1)
            V.tensor_tensor(sf[b][:, lo:lo + QP], p, T.zero[:, 0:QP], AluOpType.max).then_inc(
                sem["r%d%d" % (j, b)], 1)
    for j in range(len(far)):
        lo = QP * j
        po = banks[j][1][:, 0:QP]
        TE.wait_ge(sem["r%d0" % j], 1)
        TE.matmul(po, vb[0], sf[0][:, lo:lo + QP], True, False)
        TE.wait_ge(sem["r%d1" % j], 1)
        TE.matmul(po, vb[1], sf[1][:, lo:lo + QP], False, True).then_inc(sem["to%d" % j], 1)
        V.wait_ge(sem["to%d" % j], 1)
        V.tensor_copy(T.of[:, lo:lo + QP], po).then_inc(sem["c%d" % j], 1)
    for j in range(len(far)):
        g.wait_ge(sem["c%d" % j], 1)
    sent += _give_back(g, T, topo, core, far, T.of, QP)
    g.wait_ge(sem.sent, sent)
